import numpy as np
import ml_dtypes


def mxq(x, axis, fmt="e4m3"):
    dtype, down = {"e4m3": (ml_dtypes.float8_e4m3fn, 7), "e5m2": (ml_dtypes.float8_e5m2, 14)}[fmt]
    v = np.moveaxis(np.asarray(x, np.float32).astype(ml_dtypes.bfloat16).astype(np.float64), axis, -1)
    blocks = v.reshape(v.shape[:-1] + (-1, 32))
    amax = np.abs(blocks).max(-1, keepdims=True)
    byte = np.maximum(np.where(amax > 0, np.frexp(amax)[1] - 1 + 127, 0) - down, 1)
    scale = np.exp2(byte - 127.0)
    codes = (blocks / scale).astype(np.float32).astype(dtype).astype(np.float64)
    return np.moveaxis((codes * scale).reshape(v.shape), -1, axis)


WIDE = False


def mx_kscale(k):
    if not WIDE:
        return np.ones(k)
    levels = np.array([10, -10, 5, -5, 0])
    if k % 512:
        return np.exp2(np.random.permutation(np.resize(levels, k // 32))).repeat(32)
    a = np.empty((k // 512, 16))
    for p in range(k // 512):
        a[p, :8] = np.random.permutation(np.resize(levels, 8))
        for g in range(8):
            far = levels[np.abs(levels - a[p, g]) >= 10]
            a[p, g + 8] = far[np.random.randint(len(far))]
    return np.exp2(a.ravel()).repeat(32)


def f64(x):
    return np.asarray(x).astype(np.float64)


def striped(idx):
    return np.tile(idx.reshape(-1, 16).T, (8, 1)).astype(np.uint16)


def unstriped(offs):
    return offs[:16].T.reshape(-1).astype(np.int64)


def striped8(idx):
    return np.concatenate([x.reshape(-1, 16).T for x in idx]).astype(np.uint16)


def runs(offs, k):
    lists = np.stack([offs[16 * r : 16 * r + 16].T.reshape(-1) for r in range(8)]).astype(np.int64)
    return lists[np.arange(k) % 512 // 64]


def pack_weight(w):
    k, n = w.shape
    w = f64(np.asarray(w, np.float32).astype(ml_dtypes.bfloat16)).reshape(k // 32, 32, n)
    amax = np.abs(w).max(1)
    byte = np.clip(np.where(amax > 0, np.frexp(amax)[1] - 1 + 127 - 7, 1), 1, 254)
    scaled = (w * np.exp2(127.0 - byte)[:, None, :]).reshape(k, n).astype(np.float32)
    words = np.ascontiguousarray(scaled.reshape(k // 512, 128, 4, n).transpose(0, 1, 3, 2)).astype(ml_dtypes.float8_e4m3fn).view(np.uint8)
    return words, np.ascontiguousarray(byte.astype(np.uint8).reshape(k // 512, 16, n))


def unpack_weight(words, scales):
    g, p, n, _ = words.shape
    vals = np.ascontiguousarray(words).view(ml_dtypes.float8_e4m3fn).astype(np.float64) * np.repeat(np.exp2(scales.astype(np.float64) - 127.0), 8, axis=1)[..., None]
    return vals.transpose(0, 1, 3, 2).reshape(g * 512, n)

def planes(y):
    n, m = y.shape
    v = y.astype(np.float32).astype(ml_dtypes.bfloat16).astype(np.float64).reshape(n // 32, 32, m)
    top = np.abs(v).max(1)
    byte = np.clip(np.where(top > 0, np.frexp(top)[1] - 1 + 127 - 7, 1), 1, 254)
    codes = (v * np.exp2(127.0 - byte)[:, None, :]).reshape(n, m).astype(np.float32).astype(ml_dtypes.float8_e4m3fn).view(np.uint8)
    words = codes.reshape(n // 512, 128, 4, m).transpose(0, 1, 3, 2)
    return np.ascontiguousarray(words), np.ascontiguousarray(byte.astype(np.uint8).reshape(n // 512, 16, m))


K, T, S, H, J, W = 512, 2048, 512, 512, 512, 256


def setup_inputs():
    n = np.random.standard_normal
    s = mx_kscale(K)[:, None]
    u = mx_kscale(S)
    packed_xT = pack_weight(n((K, T)) * s)
    packed_w1 = pack_weight(n((K, H)) / np.sqrt(K) / s)
    perm = np.stack([np.random.permutation(S) for _ in range(8)])
    return {
        "x_words": packed_xT[0],
        "x_scales": packed_xT[1],
        "w1_words": packed_w1[0],
        "w1_scales": packed_w1[1],
        "tab": n((H, J)).astype(np.float32),
        "ga": (np.random.uniform(0.5, 1.5, (H, 1)) * u[:, None]).astype(np.float32),
        "gb": (np.random.uniform(0.5, 1.5, (H, 1)) / u[:, None]).astype(np.float32),
        "offs": striped(np.random.permutation(T)[:S]),
        "n1": striped8(np.stack([np.random.permutation(S) for _ in range(8)])),
        "n2": striped8(np.stack([np.random.permutation(S) for _ in range(8)])),
        "n3": striped8(np.stack([np.random.permutation(S) for _ in range(8)])),
        "n4": striped8(np.random.randint(0, J, (8, S))),
        "n5": striped8(np.stack([np.random.permutation(S) for _ in range(8)])),
        "n6": striped8(perm[:, :W]),
        "n7": striped8(perm[:, W:]),
    }


def reference(x_words, x_scales, w1_words, w1_scales, tab, ga, gb, offs, n1, n2, n3, n4, n5, n6, n7):
    xq = unpack_weight(x_words, x_scales)[:, unstriped(offs)]
    y = unpack_weight(w1_words, w1_scales).T @ xq
    st = y - (y[np.arange(H)[:, None], runs(n1, H)])
    su = np.maximum(st, st[np.arange(H)[:, None], runs(n2, H)])
    z = f64(ga) * (su + 0.5 * (su[np.arange(H)[:, None], runs(n3, H)]))
    z2 = f64(gb) * (np.maximum(y + f64(tab)[np.arange(H)[:, None], runs(n4, H)], y[np.arange(H)[:, None], runs(n5, H)]))
    s = 0.0625 * ((mxq(z, 0, "e4m3").T @ mxq(z2, 0, "e4m3")))
    pb = s[np.arange(S)[:, None], runs(n7, S)]
    pa = s[np.arange(S)[:, None], runs(n6, S)]
    rb = pb - (0.5 * pa)
    ra = np.sqrt((pa) ** 2 + (pb) ** 2 + 0.25)
    ds = np.zeros((S, S))
    ds[np.arange(S)[:, None], runs(n6, S)] = ra
    out = ds.copy()
    out[np.arange(S)[:, None], runs(n7, S)] = rb
    return (out,) + planes(out)

@@ -1,0 +1,302 @@
+from contextlib import ExitStack
+
+import concourse.mybir as mybir
+from concourse.masks import make_identity
+
+K, T, S, H, W = 512, 2048, 512, 512, 256
+P = 128
+PACK = 4
+HALF = S // 2
+FLOPS = 2 * K * H * S + 2 * H * S * S
+
+F32 = mybir.dt.float32
+BF16 = mybir.dt.bfloat16
+I32 = mybir.dt.int32
+U32 = mybir.dt.uint32
+U16 = mybir.dt.uint16
+U8 = mybir.dt.uint8
+FP8X4 = mybir.dt.float8_e4m3fn_x4
+ALU = mybir.AluOpType
+ACT = mybir.ActivationFunctionType
+
+
+def tile_picked_selfthreekindpolar_none_po_kernel(
+    tc, x_words, x_scales, w1_words, w1_scales, tab, ga, gb, offs, n1, n2, n3, n4, n5, n6, n7, out_0, out_1, out_2
+):
+    nc = tc.nc
+    tiles = range(PACK)
+    with ExitStack() as ctx:
+        keep = ctx.enter_context(tc.tile_pool(name="keep", bufs=1))
+        psum = ctx.enter_context(tc.psum_pool(name="psum", bufs=1))
+
+        def sb(name, shape, dtype):
+            return keep.tile(shape, dtype, name=name, align_bytes=64)
+
+        def bank(b, name):
+            return psum.tile([P, S], F32, name=name, tag=f"bank{b}")
+
+        l_offs, l1, l2, l3, l4, l5, l6, l7 = [
+            sb(nm, list(src.shape), U16)
+            for nm, src in (("l_offs", offs), ("l1", n1), ("l2", n2), ("l3", n3), ("l4", n4), ("l5", n5), ("l6", n6), ("l7", n7))
+        ]
+        xw = sb("xw", [P, T], I32)
+        xs = sb("xs", [P, T], U8)
+        ww = sb("ww", [P, H], I32)
+        ws = sb("ws", [P, H], U8)
+        wd = sb("wd", [P, H], I32)
+        wsd = sb("wsd", [P, H], U8)
+        xg = sb("xg", [P, S], U32)
+        xsg = sb("xsg", [P, S], U8)
+        ga_sb = sb("ga_sb", [P, PACK], F32)
+        gb_sb = sb("gb_sb", [P, PACK], F32)
+        gb_sign = sb("gb_sign", [P, PACK], F32)
+        gb_step = sb("gb_step", [P, PACK], F32)
+        gb_abs = sb("gb_abs", [P, PACK], F32)
+        ga_signed = sb("ga_signed", [P, PACK], F32)
+        ga_neg = sb("ga_neg", [P, PACK], F32)
+        ga_neg_half = sb("ga_neg_half", [P, PACK], F32)
+        ident = sb("ident", [P, P], F32)
+        y_win = [sb(f"y_win{t}", [P, 2 * S], F32) for t in tiles]
+        tab_win = [sb(f"tab_win{t}", [P, 2 * S], F32) for t in tiles]
+        nst_win = [sb(f"nst_win{t}", [P, 2 * S], F32) for t in tiles]
+        tab_rows = tab.rearrange("(p t) j -> t p j", t=PACK)
+
+        nc.gpsimd.memset(xs[:].bitcast(I32), 0)
+        nc.vector.memset(ws[:].bitcast(I32), 0)
+        nc.sync.dma_start(l_offs[:], offs)
+        for q in range(4):
+            nc.sync.dma_start(xs[32 * q : 32 * q + 4, :].bitcast(I32), x_scales[0, 4 * q : 4 * q + 4, :].bitcast(I32))
+        for q in range(4):
+            queue = nc.sync if q < 2 else nc.gpsimd
+            queue.dma_start(ws[32 * q : 32 * q + 4, :].bitcast(I32), w1_scales[0, 4 * q : 4 * q + 4, :].bitcast(I32))
+        nc.sync.dma_start(xw[:], x_words[0].rearrange("p n r -> p (n r)").bitcast(I32))
+        nc.sync.dma_start(ww[:], w1_words[0].rearrange("p n r -> p (n r)").bitcast(I32))
+        nc.sync.dma_start(l1[:], n1)
+        nc.sync.dma_start(tab_win[0][:, 0:S], tab_rows[0])
+        nc.sync.dma_start(l4[:], n4)
+        nc.sync.dma_start(l5[:], n5)
+        nc.sync.dma_start(tab_win[1][:, 0:S], tab_rows[1])
+        nc.sync.dma_start(l2[:], n2)
+        for t in range(2, PACK):
+            nc.sync.dma_start(tab_win[t][:, 0:S], tab_rows[t])
+        nc.sync.dma_start(l3[:], n3)
+        nc.sync.dma_start(l6[:], n6)
+        nc.sync.dma_start(l7[:], n7)
+        nc.gpsimd.dma_start(ga_sb[:], ga.rearrange("(p t) o -> p (t o)", t=PACK))
+        nc.gpsimd.dma_start(gb_sb[:], gb.rearrange("(p t) o -> p (t o)", t=PACK))
+        nc.vector.memset(y_win[0][:, S:], 0.0)
+        nc.scalar.copy(tab_win[0][:, S:], y_win[0][:, S:])
+        for t in range(1, PACK):
+            nc.scalar.copy(y_win[t][:, S:], y_win[0][:, S:])
+            nc.scalar.copy(tab_win[t][:, S:], y_win[0][:, S:])
+
+        make_identity(nc, ident[:])
+        nc.gpsimd.tensor_scalar(gb_step[:], gb_sb[:], 0.0, 2.0, ALU.is_ge, ALU.mult)
+        nc.gpsimd.tensor_scalar(gb_sign[:], gb_step[:], 1.0, -1.0, ALU.mult, ALU.add)
+        nc.gpsimd.tensor_tensor(gb_abs[:], gb_sb[:], gb_sign[:], ALU.mult)
+        nc.gpsimd.tensor_tensor(ga_signed[:], ga_sb[:], gb_sign[:], ALU.mult)
+        nc.gpsimd.tensor_scalar(ga_neg[:], ga_signed[:], -1.0, 0.0, ALU.mult, ALU.add)
+        nc.gpsimd.tensor_scalar(ga_neg_half[:], ga_signed[:], -0.5, 0.0, ALU.mult, ALU.add)
+
+        nc.vector.tensor_copy(xsg[:], xs[:].indirect(l_offs[:]))
+        nc.vector.tensor_copy(wsd[:].rearrange("p (t m) -> p t m", t=PACK), ws[:].rearrange("p (m t) -> p t m", t=PACK))
+
+
+        def first_product(out, t, cols):
+            rows = slice(t * P, (t + 1) * P)
+            nc.tensor.matmul_mx(
+                out=out,
+                lhsT=wd[:, rows].bitcast(FP8X4),
+                lhsT_scale=wsd[:, rows],
+                rhs=xg[:, cols].bitcast(FP8X4),
+                rhs_scale=xsg[:, cols],
+                start=True,
+                stop=True,
+            )
+
+        halves = [slice(0, HALF), slice(HALF, S)]
+        y0_ps = [bank(h, f"y0_ps{h}") for h in range(2)]
+        for h in range(2):
+            nc.vector.tensor_copy(xg[:, halves[h]], xw[:].bitcast(U32).indirect(l_offs[:, h * 16 : (h + 1) * 16]))
+            if h == 0:
+                nc.vector.tensor_copy(wd[:].rearrange("p (t m) -> p t m", t=PACK), ww[:].rearrange("p (m t) -> p t m", t=PACK))
+            first_product(y0_ps[h][:, 0:HALF], 0, halves[h])
+            nc.scalar.copy(y_win[0][:, halves[h]], y0_ps[h][:, 0:HALF])
+        for h in range(2):
+            nc.scalar.copy(nst_win[0][:, S + h * HALF : S + (h + 1) * HALF], y0_ps[h][:, 0:HALF])
+        for t in range(1, PACK):
+            y_ps = bank(t + 1, f"y_ps{t}")
+            first_product(y_ps[:], t, slice(0, S))
+            nc.scalar.copy(y_win[t][:, 0:S], y_ps[:])
+            nc.scalar.copy(nst_win[t][:, S:], y_ps[:])
+
+        zf = sb("zf", [P, PACK, S], F32)
+        a_sb = [sb(f"a_sb{t}", [P, S], F32) for t in tiles]
+        d_sb = [sb(f"d_sb{t}", [P, S], F32) for t in tiles]
+        a_scaled = [sb(f"a_scaled{t}", [P, S], F32) for t in tiles]
+        r_scaled = [sb(f"r_scaled{t}", [P, S], F32) for t in tiles]
+        g2 = [sb(f"g2_{t}", [P, S], F32) for t in tiles]
+        nsu = [sb(f"nsu{t}", [P, S], F32) for t in tiles]
+        half_win = [sb(f"half_win{t}", [P, S], F32) for t in tiles]
+        full = [sb(f"full{t}", [P, S], F32) for t in tiles]
+        z2_turned = sb("z2_turned", [P, PACK, S], BF16)
+        z2_in = sb("z2_in", [P, S, PACK], BF16)
+        z_in = sb("z_in", [P, PACK, P, PACK], BF16)
+        z2_codes = sb("z2_codes", [P, S], U32)
+        z2_scales = sb("z2_scales", [P, S], U8)
+        z_codes = sb("z_codes", [P, S], U32)
+        z_scales = sb("z_scales", [P, S], U8)
+        sum_ps = [bank((5 + b) % 8, f"sum_ps{b}") for b in tiles]
+
+        def add_turned(out, first, second):
+            nc.tensor.matmul(out, first, ident[:], start=True, stop=False, is_transpose=True)
+            nc.tensor.matmul(out, second, ident[:], start=False, stop=True, is_transpose=True)
+
+        def g4(t):
+            nc.vector.tensor_tensor(a_sb[t][:], tab_win[t][:].indirect(l4[:]), y_win[t][:, 0:S], ALU.add)
+            nc.scalar.activation(a_scaled[t][:], a_sb[t][:], ACT.Copy, scale=gb_abs[:, t : t + 1])
+
+        def g5(t):
+            nc.vector.tensor_tensor(d_sb[t][:], y_win[t][:].indirect(l5[:]), a_sb[t][:], ALU.subtract)
+            nc.scalar.activation(r_scaled[t][:], d_sb[t][:], ACT.Relu, scale=gb_abs[:, t : t + 1])
+            for b in tiles:
+                cols = slice(b * P, (b + 1) * P)
+                add_turned(sum_ps[b][:, t * P : (t + 1) * P], a_scaled[t][:, cols], r_scaled[t][:, cols])
+
+        def z2_back(pair):
+            back_ps = bank(1 + pair, f"back_ps{pair}")
+            for b in (2 * pair, 2 * pair + 1):
+                nc.scalar.copy(
+                    z2_turned[:, b, :].rearrange("j (u p e) -> j u p e", u=2, e=2),
+                    sum_ps[b][:].rearrange("j (u e p) -> j u p e", u=2, e=2),
+                )
+                words = z2_turned[:, b, :].bitcast(F32)
+                for u in range(2):
+                    at = (b % 2) * 2 * P + u * P
+                    nc.tensor.transpose(back_ps[:, at : at + P], words[:, u * P : (u + 1) * P], ident[:])
+            nc.scalar.copy(
+                z2_in[:, pair * HALF : (pair + 1) * HALF, :].rearrange("p j t -> p (j t)").bitcast(F32).rearrange("p (b j u) -> p b j u", b=2, u=2),
+                back_ps[:].rearrange("p (b u j) -> p b j u", b=2, u=2),
+            )
+
+        def g1(t):
+            nc.vector.tensor_tensor(nst_win[t][:, 0:S], y_win[t][:].indirect(l1[:]), nst_win[t][:, S:], ALU.subtract)
+
+        def g2f(t):
+            nc.vector.tensor_copy(g2[t][:], nst_win[t][:].indirect(l2[:]))
+
+        def m1(t):
+            nc.vector.tensor_tensor(nsu[t][:], nst_win[t][:, 0:S], g2[t][:], ALU.min)
+            nc.scalar.activation(half_win[t][:], nsu[t][:], ACT.Copy, scale=ga_neg_half[:, t : t + 1])
+            nc.scalar.activation(full[t][:], nsu[t][:], ACT.Copy, scale=ga_neg[:, t : t + 1])
+
+        def g3(t, h):
+            nc.vector.tensor_tensor(
+                zf[:, t, halves[h]], half_win[t][:].indirect(l3[:, h * 16 : (h + 1) * 16]), full[t][:, halves[h]], ALU.add
+            )
+
+        def quant_z2():
+            nc.vector.quantize_mx(out=z2_codes[:].bitcast(FP8X4), scales=z2_scales[:], in_=z2_in[:].rearrange("p j t -> p (j t)"))
+
+        for step in (
+            (g4, 0), (g1, 0), (g5, 0), (g4, 1), (g1, 1), (g5, 1), (g4, 2), (g2f, 0), (g5, 2), (g4, 3), (m1, 0), (g5, 3),
+            (g1, 2), (g2f, 1), (z2_back, 0), (g1, 3), (m1, 1), (z2_back, 1), (g2f, 2), (g2f, 3), (m1, 2), (g3, 0, 0), (m1, 3),
+            (g3, 1, 0), (g3, 2, 0), (quant_z2,), (g3, 3, 0),
+        ):
+            step[0](*step[1:])
+        nc.scalar.copy(
+            z_in[:, :, 0 : HALF // 4, :].rearrange("p u m t -> p m t u"),
+            zf[:, :, 0:HALF].rearrange("p t (m u) -> p m t u", u=PACK),
+        )
+        for t in tiles:
+            g3(t, 1)
+        late = zf[:, :, HALF:S].rearrange("p t (m u) -> p u m t", u=PACK)
+        nc.vector.tensor_copy(z_in[:, 0, HALF // 4 :, :], late[:, 0])
+        nc.vector.tensor_copy(z_in[:, 1, HALF // 4 :, :], late[:, 1])
+        nc.scalar.copy(z_in[:, 2:4, HALF // 4 :, :].rearrange("p u m t -> p m t u"), late[:, 2:4].rearrange("p u m t -> p m t u"))
+
+        s_win = [sb(f"s_win{t}", [P, S], F32) for t in tiles]
+
+        def second_product(out, t, cols):
+            rows = slice(t * P, (t + 1) * P)
+            nc.tensor.matmul_mx(
+                out=out,
+                lhsT=z_codes[:, rows].bitcast(FP8X4),
+                lhsT_scale=z_scales[:, rows],
+                rhs=z2_codes[:, cols].bitcast(FP8X4),
+                rhs_scale=z2_scales[:, cols],
+                start=True,
+                stop=True,
+            )
+
+        for t in tiles:
+            rows = slice(t * P, (t + 1) * P)
+            nc.vector.quantize_mx(out=z_codes[:, rows].bitcast(FP8X4), scales=z_scales[:, rows], in_=z_in[:, t].rearrange("p m t -> p (m t)"))
+        s0_ps = [bank(3 + h, f"s0_ps{h}") for h in range(2)]
+        for h in range(2):
+            second_product(s0_ps[h][:, 0:HALF], 0, halves[h])
+        nc.scalar.activation(s_win[0][:, halves[0]], s0_ps[0][:, 0:HALF], ACT.Copy, scale=0.0625)
+        nc.vector.tensor_scalar(s_win[0][:, halves[1]], s0_ps[1][:, 0:HALF], 0.0625, None, ALU.mult)
+        for t in range(1, PACK):
+            s_ps = bank(4 + t, f"s_ps{t}")
+            second_product(s_ps[:], t, slice(0, S))
+            nc.scalar.activation(s_win[t][:], s_ps[:], ACT.Copy, scale=0.0625)
+
+        nh = [sb(f"nh{t}", [P, W], F32) for t in tiles]
+        pb = [sb(f"pb{t}", [P, W], F32) for t in tiles]
+        sqa = [sb(f"sqa{t}", [P, W], F32) for t in tiles]
+        sqb = [sb(f"sqb{t}", [P, W], F32) for t in tiles]
+        ra_turned = [sb(f"ra_turned{t}", [P, W], F32) for t in tiles]
+        ra = [sb(f"ra{t}", [P, W], F32) for t in tiles]
+        o_win = [sb(f"o_win{t}", [P, S], F32) for t in tiles]
+        o_planes = sb("o_planes", [P, PACK, S], BF16)
+        o_in = sb("o_in", [P, S, PACK], BF16)
+        o_codes = sb("o_codes", [P, S], I32)
+        o_scales = sb("o_scales", [P, S], U8)
+        out_rows = out_0.rearrange("(p t) j -> t p j", t=PACK)
+
+        def fetch(t):
+            nc.vector.tensor_scalar(nh[t][:], s_win[t][:].indirect(l6[:]), -0.5, 0.0, ALU.mult, ALU.add)
+            nc.vector.tensor_copy(pb[t][:], s_win[t][:].indirect(l7[:]))
+            nc.scalar.activation(sqa[t][:], nh[t][:], ACT.Square, scale=2.0)
+            nc.scalar.activation(sqb[t][:], pb[t][:], ACT.Square)
+
+        def root(t):
+            q_ps = bank(2 * (t % 2), f"q_ps{t}")
+            ra_ps = bank(2 * (t % 2) + 1, f"ra_ps{t}")
+            for b in range(2):
+                cols = slice(b * P, (b + 1) * P)
+                add_turned(q_ps[:, cols], sqa[t][:, cols], sqb[t][:, cols])
+            nc.scalar.activation(ra_turned[t][:], q_ps[:, 0:W], ACT.Sqrt, bias=0.25)
+            for b in range(2):
+                cols = slice(b * P, (b + 1) * P)
+                nc.tensor.transpose(ra_ps[:, cols], ra_turned[t][:, cols], ident[:])
+            nc.scalar.copy(ra[t][:], ra_ps[:, 0:W])
+
+        def put_b(t):
+            nc.vector.tensor_tensor(o_win[t][:].indirect(l7[:]), pb[t][:], nh[t][:], ALU.add)
+
+        def put_a(t):
+            nc.vector.tensor_copy(o_win[t][:].indirect(l6[:]), ra[t][:])
+            nc.sync.dma_start(out_rows[t], o_win[t][:])
+            if t < PACK - 1:
+                nc.scalar.copy(o_planes[:, t, :], o_win[t][:])
+
+        for step in (
+            (fetch, 0), (fetch, 1), (root, 0), (put_b, 0), (fetch, 2), (root, 1), (put_b, 1), (fetch, 3), (root, 2), (put_a, 0),
+            (put_b, 2), (root, 3), (put_a, 1), (put_b, 3), (put_a, 2), (put_a, 3),
+        ):
+            step[0](step[1])
+        out_words = out_1[0].rearrange("p n r -> p (n r)").bitcast(I32)
+        for copy, cols in ((nc.vector.tensor_copy, halves[0]), (nc.scalar.copy, halves[1])):
+            copy(o_planes[:, PACK - 1, cols], o_win[PACK - 1][:, cols])
+            copy(
+                o_in[:, cols, :].rearrange("p (c i) t -> p c t i", i=4),
+                o_planes[:, :, cols].rearrange("p t (c i) -> p c t i", i=4),
+            )
+        for cols in halves:
+            nc.vector.quantize_mx(out=o_codes[:, cols].bitcast(FP8X4), scales=o_scales[:, cols], in_=o_in[:, cols, :].rearrange("p j t -> p (j t)"))
+            nc.sync.dma_start(out_words[:, cols], o_codes[:, cols])
+        for q in range(4):
+            queue = nc.scalar if q % 2 == 0 else nc.sync
+            queue.dma_start(out_2[0, 4 * q : 4 * q + 4, :].bitcast(I32), o_scales[32 * q : 32 * q + 4, :].bitcast(I32))

@@ -7,6 +7,10 @@ K, T, S, H, W = 512, 2048, 512, 512, 256
 P = 128
 PACK = 4
 HALF = S // 2
+LIST_ROWS = 16
+QUADS = 4
+X_EARLY = 512
+VECTOR_COLUMNS = 320
 FLOPS = 2 * K * H * S + 2 * H * S * S
 
 F32 = mybir.dt.float32
@@ -25,278 +29,342 @@ def tile_picked_selfthreekindpolar_none_po_kernel(
 ):
     nc = tc.nc
     tiles = range(PACK)
+    last = PACK - 1
+    halves = [slice(0, HALF), slice(HALF, S)]
+    list_halves = [slice(0, HALF // LIST_ROWS), slice(HALF // LIST_ROWS, S // LIST_ROWS)]
+    blocks = [slice(b * P, (b + 1) * P) for b in tiles]
+
     with ExitStack() as ctx:
         keep = ctx.enter_context(tc.tile_pool(name="keep", bufs=1))
         psum = ctx.enter_context(tc.psum_pool(name="psum", bufs=1))
 
-        def sb(name, shape, dtype):
-            return keep.tile(shape, dtype, name=name, align_bytes=64)
+        def sb(name, shape, dtype, reuse=None):
+            return keep.tile(shape, dtype, name=name, tag=reuse or name, align_bytes=64)
 
-        def bank(b, name):
-            return psum.tile([P, S], F32, name=name, tag=f"bank{b}")
+        def bank(number, name):
+            return psum.tile([P, S], F32, name=name, tag=f"bank{number}")
 
-        l_offs, l1, l2, l3, l4, l5, l6, l7 = [
-            sb(nm, list(src.shape), U16)
-            for nm, src in (("l_offs", offs), ("l1", n1), ("l2", n2), ("l3", n3), ("l4", n4), ("l5", n5), ("l6", n6), ("l7", n7))
+        def product(out, stationary, stationary_scales, moving, moving_scales):
+            nc.tensor.matmul_mx(
+                out=out,
+                lhsT=stationary.bitcast(FP8X4),
+                lhsT_scale=stationary_scales,
+                rhs=moving.bitcast(FP8X4),
+                rhs_scale=moving_scales,
+                start=True,
+                stop=True,
+            )
+
+        def add_turned(out, first, second):
+            nc.tensor.matmul(out, first, ident[:], start=True, stop=False, is_transpose=True)
+            nc.tensor.matmul(out, second, ident[:], start=False, stop=True, is_transpose=True)
+
+        offs_sb, n1_sb, n2_sb, n3_sb, n4_sb, n5_sb, n6_sb, n7_sb = [
+            sb(name, list(src.shape), U16)
+            for name, src in (
+                ("offs_sb", offs), ("n1_sb", n1), ("n2_sb", n2), ("n3_sb", n3),
+                ("n4_sb", n4), ("n5_sb", n5), ("n6_sb", n6), ("n7_sb", n7),
+            )
         ]
         xw = sb("xw", [P, T], I32)
         xs = sb("xs", [P, T], U8)
         ww = sb("ww", [P, H], I32)
         ws = sb("ws", [P, H], U8)
-        wd = sb("wd", [P, H], I32)
-        wsd = sb("wsd", [P, H], U8)
-        xg = sb("xg", [P, S], U32)
-        xsg = sb("xsg", [P, S], U8)
         ga_sb = sb("ga_sb", [P, PACK], F32)
         gb_sb = sb("gb_sb", [P, PACK], F32)
-        gb_sign = sb("gb_sign", [P, PACK], F32)
-        gb_step = sb("gb_step", [P, PACK], F32)
-        gb_abs = sb("gb_abs", [P, PACK], F32)
-        ga_signed = sb("ga_signed", [P, PACK], F32)
-        ga_neg = sb("ga_neg", [P, PACK], F32)
-        ga_neg_half = sb("ga_neg_half", [P, PACK], F32)
-        ident = sb("ident", [P, P], F32)
         y_win = [sb(f"y_win{t}", [P, 2 * S], F32) for t in tiles]
         tab_win = [sb(f"tab_win{t}", [P, 2 * S], F32) for t in tiles]
         nst_win = [sb(f"nst_win{t}", [P, 2 * S], F32) for t in tiles]
+        y_copy = [nst_win[t][:, S:] for t in tiles]
+        x_rows = x_words[0].rearrange("p n r -> p (n r)").bitcast(I32)
         tab_rows = tab.rearrange("(p t) j -> t p j", t=PACK)
 
         nc.gpsimd.memset(xs[:].bitcast(I32), 0)
         nc.vector.memset(ws[:].bitcast(I32), 0)
-        nc.sync.dma_start(l_offs[:], offs)
-        for q in range(4):
-            nc.sync.dma_start(xs[32 * q : 32 * q + 4, :].bitcast(I32), x_scales[0, 4 * q : 4 * q + 4, :].bitcast(I32))
-        for q in range(4):
-            queue = nc.sync if q < 2 else nc.gpsimd
-            queue.dma_start(ws[32 * q : 32 * q + 4, :].bitcast(I32), w1_scales[0, 4 * q : 4 * q + 4, :].bitcast(I32))
-        nc.sync.dma_start(xw[:], x_words[0].rearrange("p n r -> p (n r)").bitcast(I32))
+        nc.sync.dma_start(offs_sb[:], offs)
         nc.sync.dma_start(ww[:], w1_words[0].rearrange("p n r -> p (n r)").bitcast(I32))
-        nc.sync.dma_start(l1[:], n1)
+        nc.sync.dma_start(xw[:, 0:X_EARLY], x_rows[:, 0:X_EARLY])
+        for q in range(QUADS):
+            nc.sync.dma_start(xs[32 * q : 32 * q + 4, :].bitcast(I32), x_scales[0, 4 * q : 4 * q + 4, :].bitcast(I32))
+        nc.sync.dma_start(xw[:, X_EARLY:], x_rows[:, X_EARLY:])
+        for q in range(QUADS):
+            nc.sync.dma_start(ws[32 * q : 32 * q + 4, :].bitcast(I32), w1_scales[0, 4 * q : 4 * q + 4, :].bitcast(I32))
         nc.sync.dma_start(tab_win[0][:, 0:S], tab_rows[0])
-        nc.sync.dma_start(l4[:], n4)
-        nc.sync.dma_start(l5[:], n5)
+        nc.sync.dma_start(n4_sb[:], n4)
+        nc.sync.dma_start(n1_sb[:], n1)
+        nc.sync.dma_start(n5_sb[:], n5)
         nc.sync.dma_start(tab_win[1][:, 0:S], tab_rows[1])
-        nc.sync.dma_start(l2[:], n2)
+        nc.sync.dma_start(n2_sb[:], n2)
         for t in range(2, PACK):
             nc.sync.dma_start(tab_win[t][:, 0:S], tab_rows[t])
-        nc.sync.dma_start(l3[:], n3)
-        nc.sync.dma_start(l6[:], n6)
-        nc.sync.dma_start(l7[:], n7)
-        nc.gpsimd.dma_start(ga_sb[:], ga.rearrange("(p t) o -> p (t o)", t=PACK))
+        nc.sync.dma_start(n3_sb[:], n3)
+        nc.sync.dma_start(n6_sb[:], n6)
+        nc.sync.dma_start(n7_sb[:], n7)
         nc.gpsimd.dma_start(gb_sb[:], gb.rearrange("(p t) o -> p (t o)", t=PACK))
+        nc.gpsimd.dma_start(ga_sb[:], ga.rearrange("(p t) o -> p (t o)", t=PACK))
         nc.vector.memset(y_win[0][:, S:], 0.0)
         nc.scalar.copy(tab_win[0][:, S:], y_win[0][:, S:])
         for t in range(1, PACK):
             nc.scalar.copy(y_win[t][:, S:], y_win[0][:, S:])
             nc.scalar.copy(tab_win[t][:, S:], y_win[0][:, S:])
 
+        ident = sb("ident", [P, P], F32)
+        gb_step, gb_sign, gb_abs, ga_signed, ga_half, ga_neg, ga_neg_half = [
+            sb(name, [P, PACK], F32)
+            for name in ("gb_step", "gb_sign", "gb_abs", "ga_signed", "ga_half", "ga_neg", "ga_neg_half")
+        ]
         make_identity(nc, ident[:])
         nc.gpsimd.tensor_scalar(gb_step[:], gb_sb[:], 0.0, 2.0, ALU.is_ge, ALU.mult)
         nc.gpsimd.tensor_scalar(gb_sign[:], gb_step[:], 1.0, -1.0, ALU.mult, ALU.add)
         nc.gpsimd.tensor_tensor(gb_abs[:], gb_sb[:], gb_sign[:], ALU.mult)
         nc.gpsimd.tensor_tensor(ga_signed[:], ga_sb[:], gb_sign[:], ALU.mult)
+        nc.gpsimd.tensor_scalar(ga_half[:], ga_signed[:], 0.5, 0.0, ALU.mult, ALU.add)
         nc.gpsimd.tensor_scalar(ga_neg[:], ga_signed[:], -1.0, 0.0, ALU.mult, ALU.add)
         nc.gpsimd.tensor_scalar(ga_neg_half[:], ga_signed[:], -0.5, 0.0, ALU.mult, ALU.add)
 
-        nc.vector.tensor_copy(xsg[:], xs[:].indirect(l_offs[:]))
-        nc.vector.tensor_copy(wsd[:].rearrange("p (t m) -> p t m", t=PACK), ws[:].rearrange("p (m t) -> p t m", t=PACK))
-
-
-        def first_product(out, t, cols):
-            rows = slice(t * P, (t + 1) * P)
-            nc.tensor.matmul_mx(
-                out=out,
-                lhsT=wd[:, rows].bitcast(FP8X4),
-                lhsT_scale=wsd[:, rows],
-                rhs=xg[:, cols].bitcast(FP8X4),
-                rhs_scale=xsg[:, cols],
-                start=True,
-                stop=True,
-            )
-
-        halves = [slice(0, HALF), slice(HALF, S)]
-        y0_ps = [bank(h, f"y0_ps{h}") for h in range(2)]
+        picked = sb("picked", [P, S], U32)
+        picked_scales = sb("picked_scales", [P, S], U8)
+        w_dealt = sb("w_dealt", [P, PACK, P], I32)
+        ws_first = sb("ws_first", [P, P], U8)
+        ws_rest = sb("ws_rest", [P, last, P], U8)
+        ws_by_tile = ws[:].rearrange("p (m t) -> p t m", t=PACK)
+        nc.vector.tensor_copy(picked_scales[:], xs[:].indirect(offs_sb[:]))
+        nc.vector.tensor_copy(w_dealt[:], ww[:].rearrange("p (m t) -> p t m", t=PACK))
+        y_first = [bank(h, f"y_first{h}") for h in range(2)]
+        nc.vector.tensor_copy(picked[:, halves[0]], xw[:].bitcast(U32).indirect(offs_sb[:, list_halves[0]]))
+        nc.vector.tensor_copy(ws_first[:], ws_by_tile[:, 0])
+        product(y_first[0][:, 0:HALF], w_dealt[:, 0], ws_first[:], picked[:, halves[0]], picked_scales[:, halves[0]])
+        nc.scalar.copy(y_win[0][:, halves[0]], y_first[0][:, 0:HALF])
+        nc.vector.tensor_copy(picked[:, halves[1]], xw[:].bitcast(U32).indirect(offs_sb[:, list_halves[1]]))
+        product(y_first[1][:, 0:HALF], w_dealt[:, 0], ws_first[:], picked[:, halves[1]], picked_scales[:, halves[1]])
+        nc.scalar.copy(y_win[0][:, halves[1]], y_first[1][:, 0:HALF])
         for h in range(2):
-            nc.vector.tensor_copy(xg[:, halves[h]], xw[:].bitcast(U32).indirect(l_offs[:, h * 16 : (h + 1) * 16]))
-            if h == 0:
-                nc.vector.tensor_copy(wd[:].rearrange("p (t m) -> p t m", t=PACK), ww[:].rearrange("p (m t) -> p t m", t=PACK))
-            first_product(y0_ps[h][:, 0:HALF], 0, halves[h])
-            nc.scalar.copy(y_win[0][:, halves[h]], y0_ps[h][:, 0:HALF])
-        for h in range(2):
-            nc.scalar.copy(nst_win[0][:, S + h * HALF : S + (h + 1) * HALF], y0_ps[h][:, 0:HALF])
+            nc.scalar.copy(y_copy[0][:, halves[h]], y_first[h][:, 0:HALF])
+        nc.vector.tensor_copy(ws_rest[:], ws_by_tile[:, 1:])
+        y_ps = {t: bank(t + 1, f"y_ps{t}") for t in range(1, PACK)}
         for t in range(1, PACK):
-            y_ps = bank(t + 1, f"y_ps{t}")
-            first_product(y_ps[:], t, slice(0, S))
-            nc.scalar.copy(y_win[t][:, 0:S], y_ps[:])
-            nc.scalar.copy(nst_win[t][:, S:], y_ps[:])
+            product(y_ps[t][:], w_dealt[:, t], ws_rest[:, t - 1], picked[:], picked_scales[:])
 
-        zf = sb("zf", [P, PACK, S], F32)
-        a_sb = [sb(f"a_sb{t}", [P, S], F32) for t in tiles]
-        d_sb = [sb(f"d_sb{t}", [P, S], F32) for t in tiles]
+        def y_out(t):
+            nc.scalar.copy(y_win[t][:, 0:S], y_ps[t][:])
+            nc.sync.dma_start(y_copy[t], y_win[t][:, 0:S])
+
+        a = [sb(f"a{t}", [P, S], F32) for t in tiles]
         a_scaled = [sb(f"a_scaled{t}", [P, S], F32) for t in tiles]
-        r_scaled = [sb(f"r_scaled{t}", [P, S], F32) for t in tiles]
-        g2 = [sb(f"g2_{t}", [P, S], F32) for t in tiles]
-        nsu = [sb(f"nsu{t}", [P, S], F32) for t in tiles]
-        half_win = [sb(f"half_win{t}", [P, S], F32) for t in tiles]
-        full = [sb(f"full{t}", [P, S], F32) for t in tiles]
-        z2_turned = sb("z2_turned", [P, PACK, S], BF16)
+        excess = [sb(f"excess{t}", [P, S], F32) for t in tiles]
+        excess_scaled = [sb(f"excess_scaled{t}", [P, S], F32) for t in tiles]
+        z2_sum = [bank((5 + b) % 8, f"z2_sum{b}") for b in tiles]
         z2_in = sb("z2_in", [P, S, PACK], BF16)
-        z_in = sb("z_in", [P, PACK, P, PACK], BF16)
         z2_codes = sb("z2_codes", [P, S], U32)
         z2_scales = sb("z2_scales", [P, S], U8)
-        z_codes = sb("z_codes", [P, S], U32)
-        z_scales = sb("z_scales", [P, S], U8)
-        sum_ps = [bank((5 + b) % 8, f"sum_ps{b}") for b in tiles]
 
-        def add_turned(out, first, second):
-            nc.tensor.matmul(out, first, ident[:], start=True, stop=False, is_transpose=True)
-            nc.tensor.matmul(out, second, ident[:], start=False, stop=True, is_transpose=True)
+        def look_n4(t):
+            nc.vector.tensor_tensor(a[t][:], tab_win[t][:].indirect(n4_sb[:]), y_win[t][:, 0:S], ALU.add)
+            nc.scalar.activation(a_scaled[t][:], a[t][:], ACT.Copy, scale=gb_abs[:, t : t + 1])
 
-        def g4(t):
-            nc.vector.tensor_tensor(a_sb[t][:], tab_win[t][:].indirect(l4[:]), y_win[t][:, 0:S], ALU.add)
-            nc.scalar.activation(a_scaled[t][:], a_sb[t][:], ACT.Copy, scale=gb_abs[:, t : t + 1])
+        def look_n5(t):
+            nc.vector.tensor_tensor(excess[t][:], y_win[t][:].indirect(n5_sb[:]), a[t][:], ALU.subtract)
 
-        def g5(t):
-            nc.vector.tensor_tensor(d_sb[t][:], y_win[t][:].indirect(l5[:]), a_sb[t][:], ALU.subtract)
-            nc.scalar.activation(r_scaled[t][:], d_sb[t][:], ACT.Relu, scale=gb_abs[:, t : t + 1])
+        def z2_add(t):
+            nc.scalar.activation(excess_scaled[t][:], excess[t][:], ACT.Relu, scale=gb_abs[:, t : t + 1])
             for b in tiles:
-                cols = slice(b * P, (b + 1) * P)
-                add_turned(sum_ps[b][:, t * P : (t + 1) * P], a_scaled[t][:, cols], r_scaled[t][:, cols])
+                add_turned(z2_sum[b][:, blocks[t]], a_scaled[t][:, blocks[b]], excess_scaled[t][:, blocks[b]])
 
-        def z2_back(pair):
-            back_ps = bank(1 + pair, f"back_ps{pair}")
-            for b in (2 * pair, 2 * pair + 1):
+        def z2_turn_back(h):
+            turned = sb(f"z2_turned{h}", [P, 2, S], BF16)
+            back = bank(5 + 2 * h, f"z2_back{h}")
+            for b in range(2):
                 nc.scalar.copy(
-                    z2_turned[:, b, :].rearrange("j (u p e) -> j u p e", u=2, e=2),
-                    sum_ps[b][:].rearrange("j (u e p) -> j u p e", u=2, e=2),
+                    turned[:, b, :].rearrange("j (u p e) -> j u p e", u=2, e=2),
+                    z2_sum[2 * h + b][:].rearrange("j (u e p) -> j u p e", u=2, e=2),
                 )
-                words = z2_turned[:, b, :].bitcast(F32)
+                words = turned[:, b, :].bitcast(F32)
                 for u in range(2):
-                    at = (b % 2) * 2 * P + u * P
-                    nc.tensor.transpose(back_ps[:, at : at + P], words[:, u * P : (u + 1) * P], ident[:])
+                    nc.tensor.transpose(back[:, blocks[2 * b + u]], words[:, blocks[u]], ident[:])
+            z2_words = z2_in[:, halves[h], :].rearrange("p j t -> p (j t)").bitcast(F32)
             nc.scalar.copy(
-                z2_in[:, pair * HALF : (pair + 1) * HALF, :].rearrange("p j t -> p (j t)").bitcast(F32).rearrange("p (b j u) -> p b j u", b=2, u=2),
-                back_ps[:].rearrange("p (b u j) -> p b j u", b=2, u=2),
+                z2_words.rearrange("p (b j u) -> p b j u", b=2, u=2),
+                back[:].rearrange("p (b u j) -> p b j u", b=2, u=2),
             )
 
-        def g1(t):
-            nc.vector.tensor_tensor(nst_win[t][:, 0:S], y_win[t][:].indirect(l1[:]), nst_win[t][:, S:], ALU.subtract)
+        su_half = [sb(f"su_half{t}", [P, S], F32) for t in tiles]
+        su_full = [sb(f"su_full{t}", [P, S], F32) for t in tiles]
+        z_rows = [sb(f"z_rows{h}", [P, PACK, HALF], F32) for h in range(2)]
+        nst_n2 = {}
 
-        def g2f(t):
-            nc.vector.tensor_copy(g2[t][:], nst_win[t][:].indirect(l2[:]))
+        def look_n1(t):
+            nc.vector.tensor_tensor(nst_win[t][:, 0:S], y_win[t][:].indirect(n1_sb[:]), y_copy[t], ALU.subtract)
 
-        def m1(t):
-            nc.vector.tensor_tensor(nsu[t][:], nst_win[t][:, 0:S], g2[t][:], ALU.min)
-            nc.scalar.activation(half_win[t][:], nsu[t][:], ACT.Copy, scale=ga_neg_half[:, t : t + 1])
-            nc.scalar.activation(full[t][:], nsu[t][:], ACT.Copy, scale=ga_neg[:, t : t + 1])
+        def look_n2(t, reuse=None):
+            nst_n2[t] = sb(f"nst_n2_{t}", [P, S], F32, reuse)
+            nc.vector.tensor_copy(nst_n2[t][:], nst_win[t][:].indirect(n2_sb[:]))
 
-        def g3(t, h):
+        def su_by_vector(t, nsu):
+            nc.vector.tensor_tensor(nsu, nst_win[t][:, 0:S], nst_n2[t][:], ALU.min)
+            nc.scalar.activation(su_half[t][:], nsu, ACT.Copy, scale=ga_neg_half[:, t : t + 1])
+            nc.scalar.activation(su_full[t][:], nsu, ACT.Copy, scale=ga_neg[:, t : t + 1])
+
+        def look_n3(t, h):
             nc.vector.tensor_tensor(
-                zf[:, t, halves[h]], half_win[t][:].indirect(l3[:, h * 16 : (h + 1) * 16]), full[t][:, halves[h]], ALU.add
+                z_rows[h][:, t, :], su_half[t][:].indirect(n3_sb[:, list_halves[h]]), su_full[t][:, halves[h]], ALU.add
             )
 
-        def quant_z2():
-            nc.vector.quantize_mx(out=z2_codes[:].bitcast(FP8X4), scales=z2_scales[:], in_=z2_in[:].rearrange("p j t -> p (j t)"))
+        st0 = sb("st0", [P, S], F32)
+        deficit0 = sb("deficit0", [P, S], F32)
+        lift0 = sb("lift0", [P, S], F32)
+        su0_turned = sb("su0_turned", [P, S], F32)
 
-        for step in (
-            (g4, 0), (g1, 0), (g5, 0), (g4, 1), (g1, 1), (g5, 1), (g4, 2), (g2f, 0), (g5, 2), (g4, 3), (m1, 0), (g5, 3),
-            (g1, 2), (g2f, 1), (z2_back, 0), (g1, 3), (m1, 1), (z2_back, 1), (g2f, 2), (g2f, 3), (m1, 2), (g3, 0, 0), (m1, 3),
-            (g3, 1, 0), (g3, 2, 0), (quant_z2,), (g3, 3, 0),
-        ):
-            step[0](*step[1:])
-        nc.scalar.copy(
-            z_in[:, :, 0 : HALF // 4, :].rearrange("p u m t -> p m t u"),
-            zf[:, :, 0:HALF].rearrange("p t (m u) -> p m t u", u=PACK),
-        )
+        y_out(1)
+        y_out(2)
+        look_n4(0)
+        look_n1(0)
+        nc.scalar.activation(st0[:], nst_win[0][:, 0:S], ACT.Copy, scale=-1.0)
+        y_out(3)
+        look_n4(1)
+        look_n5(0)
+        z2_add(0)
+        nc.vector.tensor_tensor(deficit0[:], nst_win[0][:].indirect(n2_sb[:]), st0[:], ALU.add)
+        nc.scalar.activation(lift0[:], deficit0[:], ACT.Relu, scale=-1.0)
+        su0_sum = bank(1, "su0_sum")
+        for b in tiles:
+            add_turned(su0_sum[:, blocks[b]], st0[:, blocks[b]], lift0[:, blocks[b]])
+        look_n5(1)
+        z2_add(1)
+        look_n4(2)
+        su0_back = bank(2, "su0_back")
+        nc.scalar.copy(su0_turned[:], su0_sum[:])
+        for b in tiles:
+            nc.tensor.transpose(su0_back[:, blocks[b]], su0_turned[:, blocks[b]], ident[:])
+        look_n1(1)
+        look_n5(2)
+        nc.scalar.activation(su_half[0][:], su0_back[:], ACT.Copy, scale=ga_half[:, 0:1])
+        nc.scalar.activation(su_full[0][:], su0_back[:], ACT.Copy, scale=ga_signed[:, 0:1])
+        z2_add(2)
+        look_n4(3)
+        look_n2(1)
+        look_n5(3)
+        z2_add(3)
+        look_n1(2)
+        z2_turn_back(0)
+        look_n1(3)
+        su_by_vector(1, sb("nsu1", [P, S], F32, f"excess_scaled{last}")[:])
+        z2_turn_back(1)
+        look_n2(2, f"a_scaled{last}")
+        look_n2(3, "z2_turned0")
+        su_by_vector(2, sb("nsu2", [P, S], F32)[:])
+        look_n3(0, 0)
+        su_by_vector(3, z_rows[1][:].rearrange("p t j -> p (t j)")[:, S:])
+        look_n3(1, 0)
+        look_n3(2, 0)
+        nc.vector.quantize_mx(out=z2_codes[:].bitcast(FP8X4), scales=z2_scales[:], in_=z2_in[:].rearrange("p j t -> p (j t)"))
+        look_n3(3, 0)
+
+        z_in = [sb(f"z_in{i}", [P, 2, P, PACK], BF16) for i in range(2)]
+        z_parts = [z_rows[h][:].rearrange("p t (m u) -> p u m t", u=PACK) for h in range(2)]
+        places = [slice(0, P // 2), slice(P // 2, P)]
+
+        def deal_by_scalar(h, i):
+            nc.scalar.copy(
+                z_in[i][:, :, places[h], :].rearrange("p u m t -> p m t u"),
+                z_parts[h][:, 2 * i : 2 * i + 2].rearrange("p u m t -> p m t u"),
+            )
+
+        deal_by_scalar(0, 0)
+        deal_by_scalar(0, 1)
         for t in tiles:
-            g3(t, 1)
-        late = zf[:, :, HALF:S].rearrange("p t (m u) -> p u m t", u=PACK)
-        nc.vector.tensor_copy(z_in[:, 0, HALF // 4 :, :], late[:, 0])
-        nc.vector.tensor_copy(z_in[:, 1, HALF // 4 :, :], late[:, 1])
-        nc.scalar.copy(z_in[:, 2:4, HALF // 4 :, :].rearrange("p u m t -> p m t u"), late[:, 2:4].rearrange("p u m t -> p m t u"))
+            look_n3(t, 1)
+        for u in range(2):
+            nc.vector.tensor_copy(z_in[0][:, u, places[1], :], z_parts[1][:, u])
+        deal_by_scalar(1, 1)
 
+        z_codes = [sb(f"z_codes{u}", [P, P], U32) for u in tiles]
+        z_scales = [sb(f"z_scales{u}", [P, P], U8) for u in tiles]
         s_win = [sb(f"s_win{t}", [P, S], F32) for t in tiles]
-
-        def second_product(out, t, cols):
-            rows = slice(t * P, (t + 1) * P)
-            nc.tensor.matmul_mx(
-                out=out,
-                lhsT=z_codes[:, rows].bitcast(FP8X4),
-                lhsT_scale=z_scales[:, rows],
-                rhs=z2_codes[:, cols].bitcast(FP8X4),
-                rhs_scale=z2_scales[:, cols],
-                start=True,
-                stop=True,
+        for u in tiles:
+            nc.vector.quantize_mx(
+                out=z_codes[u][:].bitcast(FP8X4), scales=z_scales[u][:], in_=z_in[u // 2][:, u % 2].rearrange("p m t -> p (m t)")
             )
-
-        for t in tiles:
-            rows = slice(t * P, (t + 1) * P)
-            nc.vector.quantize_mx(out=z_codes[:, rows].bitcast(FP8X4), scales=z_scales[:, rows], in_=z_in[:, t].rearrange("p m t -> p (m t)"))
-        s0_ps = [bank(3 + h, f"s0_ps{h}") for h in range(2)]
+        s_first = [bank(number, f"s_first{h}") for h, number in enumerate((6, 0))]
         for h in range(2):
-            second_product(s0_ps[h][:, 0:HALF], 0, halves[h])
-        nc.scalar.activation(s_win[0][:, halves[0]], s0_ps[0][:, 0:HALF], ACT.Copy, scale=0.0625)
-        nc.vector.tensor_scalar(s_win[0][:, halves[1]], s0_ps[1][:, 0:HALF], 0.0625, None, ALU.mult)
-        for t in range(1, PACK):
-            s_ps = bank(4 + t, f"s_ps{t}")
-            second_product(s_ps[:], t, slice(0, S))
+            product(s_first[h][:, 0:HALF], z_codes[0][:], z_scales[0][:], z2_codes[:, halves[h]], z2_scales[:, halves[h]])
+        nc.scalar.activation(s_win[0][:, halves[0]], s_first[0][:, 0:HALF], ACT.Copy, scale=0.0625)
+        nc.vector.tensor_scalar(s_win[0][:, halves[1]], s_first[1][:, 0:HALF], 0.0625, None, ALU.mult)
+        for t, number in zip(range(1, PACK), (5, 7, 1)):
+            s_ps = bank(number, f"s_ps{t}")
+            product(s_ps[:], z_codes[t][:], z_scales[t][:], z2_codes[:], z2_scales[:])
             nc.scalar.activation(s_win[t][:], s_ps[:], ACT.Copy, scale=0.0625)
 
-        nh = [sb(f"nh{t}", [P, W], F32) for t in tiles]
+        pa_neg_half = [sb(f"pa_neg_half{t}", [P, W], F32) for t in tiles]
         pb = [sb(f"pb{t}", [P, W], F32) for t in tiles]
-        sqa = [sb(f"sqa{t}", [P, W], F32) for t in tiles]
-        sqb = [sb(f"sqb{t}", [P, W], F32) for t in tiles]
+        pa_square = [sb(f"pa_square{t}", [P, W], F32) for t in tiles]
+        pb_square = [sb(f"pb_square{t}", [P, W], F32) for t in tiles]
         ra_turned = [sb(f"ra_turned{t}", [P, W], F32) for t in tiles]
         ra = [sb(f"ra{t}", [P, W], F32) for t in tiles]
-        o_win = [sb(f"o_win{t}", [P, S], F32) for t in tiles]
-        o_planes = sb("o_planes", [P, PACK, S], BF16)
-        o_in = sb("o_in", [P, S, PACK], BF16)
-        o_codes = sb("o_codes", [P, S], I32)
-        o_scales = sb("o_scales", [P, S], U8)
+        out_win = [sb(f"out_win{t}", [P, S], F32) for t in tiles]
         out_rows = out_0.rearrange("(p t) j -> t p j", t=PACK)
+        ra_ps = {}
 
-        def fetch(t):
-            nc.vector.tensor_scalar(nh[t][:], s_win[t][:].indirect(l6[:]), -0.5, 0.0, ALU.mult, ALU.add)
-            nc.vector.tensor_copy(pb[t][:], s_win[t][:].indirect(l7[:]))
-            nc.scalar.activation(sqa[t][:], nh[t][:], ACT.Square, scale=2.0)
-            nc.scalar.activation(sqb[t][:], pb[t][:], ACT.Square)
+        def look_pairs(t):
+            nc.vector.tensor_scalar(pa_neg_half[t][:], s_win[t][:].indirect(n6_sb[:]), -0.5, 0.0, ALU.mult, ALU.add)
+            nc.vector.tensor_copy(pb[t][:], s_win[t][:].indirect(n7_sb[:]))
+            nc.scalar.activation(pa_square[t][:], pa_neg_half[t][:], ACT.Square, scale=2.0)
+            nc.scalar.activation(pb_square[t][:], pb[t][:], ACT.Square)
 
         def root(t):
-            q_ps = bank(2 * (t % 2), f"q_ps{t}")
-            ra_ps = bank(2 * (t % 2) + 1, f"ra_ps{t}")
-            for b in range(2):
-                cols = slice(b * P, (b + 1) * P)
-                add_turned(q_ps[:, cols], sqa[t][:, cols], sqb[t][:, cols])
-            nc.scalar.activation(ra_turned[t][:], q_ps[:, 0:W], ACT.Sqrt, bias=0.25)
-            for b in range(2):
-                cols = slice(b * P, (b + 1) * P)
-                nc.tensor.transpose(ra_ps[:, cols], ra_turned[t][:, cols], ident[:])
-            nc.scalar.copy(ra[t][:], ra_ps[:, 0:W])
+            squares = bank((2, 4)[t % 2], f"squares{t}")
+            ra_ps[t] = bank((3, 6)[t % 2], f"ra_ps{t}")
+            for b in range(W // P):
+                add_turned(squares[:, blocks[b]], pa_square[t][:, blocks[b]], pb_square[t][:, blocks[b]])
+            nc.scalar.activation(ra_turned[t][:], squares[:, 0:W], ACT.Sqrt, bias=0.25)
+            for b in range(W // P):
+                nc.tensor.transpose(ra_ps[t][:, blocks[b]], ra_turned[t][:, blocks[b]], ident[:])
 
-        def put_b(t):
-            nc.vector.tensor_tensor(o_win[t][:].indirect(l7[:]), pb[t][:], nh[t][:], ALU.add)
+        def root_out(t):
+            nc.scalar.copy(ra[t][:], ra_ps[t][:, 0:W])
 
-        def put_a(t):
-            nc.vector.tensor_copy(o_win[t][:].indirect(l6[:]), ra[t][:])
-            nc.sync.dma_start(out_rows[t], o_win[t][:])
-            if t < PACK - 1:
-                nc.scalar.copy(o_planes[:, t, :], o_win[t][:])
+        def put_rb(t):
+            nc.vector.tensor_tensor(out_win[t][:].indirect(n7_sb[:]), pb[t][:], pa_neg_half[t][:], ALU.add)
 
-        for step in (
-            (fetch, 0), (fetch, 1), (root, 0), (put_b, 0), (fetch, 2), (root, 1), (put_b, 1), (fetch, 3), (root, 2), (put_a, 0),
-            (put_b, 2), (root, 3), (put_a, 1), (put_b, 3), (put_a, 2), (put_a, 3),
-        ):
-            step[0](step[1])
+        look_pairs(0)
+        for t in range(last):
+            look_pairs(t + 1)
+            root(t)
+            put_rb(t)
+            root_out(t)
+        root(last)
+        root_out(last)
+        put_rb(last)
+
+        out_bf16 = sb("out_bf16", [P, PACK, S], BF16, f"ra_turned{last}")
+        for t in tiles:
+            nc.vector.tensor_copy(out_win[t][:].indirect(n6_sb[:]), ra[t][:])
+            nc.sync.dma_start(out_rows[t], out_win[t][:])
+            if t < last:
+                nc.scalar.copy(out_bf16[:, t, :], out_win[t][:])
+
+        out_in = [sb(f"out_in{h}", [P, HALF, PACK], BF16) for h in range(2)]
+        out_codes = sb("out_codes", [P, S], I32)
+        out_scales = sb("out_scales", [P, S], U8)
         out_words = out_1[0].rearrange("p n r -> p (n r)").bitcast(I32)
-        for copy, cols in ((nc.vector.tensor_copy, halves[0]), (nc.scalar.copy, halves[1])):
-            copy(o_planes[:, PACK - 1, cols], o_win[PACK - 1][:, cols])
+
+        def interleave(copy, h, start, stop):
             copy(
-                o_in[:, cols, :].rearrange("p (c i) t -> p c t i", i=4),
-                o_planes[:, :, cols].rearrange("p t (c i) -> p c t i", i=4),
+                out_in[h][:, start - h * HALF : stop - h * HALF, :].rearrange("p (c i) t -> p c t i", i=4),
+                out_bf16[:, :, start:stop].rearrange("p t (c i) -> p c t i", i=4),
             )
-        for cols in halves:
-            nc.vector.quantize_mx(out=o_codes[:, cols].bitcast(FP8X4), scales=o_scales[:, cols], in_=o_in[:, cols, :].rearrange("p j t -> p (j t)"))
-            nc.sync.dma_start(out_words[:, cols], o_codes[:, cols])
-        for q in range(4):
-            queue = nc.scalar if q % 2 == 0 else nc.sync
-            queue.dma_start(out_2[0, 4 * q : 4 * q + 4, :].bitcast(I32), o_scales[32 * q : 32 * q + 4, :].bitcast(I32))
+
+        nc.vector.tensor_copy(out_bf16[:, last, 0:VECTOR_COLUMNS], out_win[last][:, 0:VECTOR_COLUMNS])
+        nc.scalar.copy(out_bf16[:, last, VECTOR_COLUMNS:], out_win[last][:, VECTOR_COLUMNS:])
+        interleave(nc.vector.tensor_copy, 0, 0, HALF)
+        interleave(nc.vector.tensor_copy, 1, HALF, VECTOR_COLUMNS)
+        interleave(nc.scalar.copy, 1, VECTOR_COLUMNS, S)
+        for h in range(2):
+            nc.vector.quantize_mx(
+                out=out_codes[:, halves[h]].bitcast(FP8X4),
+                scales=out_scales[:, halves[h]],
+                in_=out_in[h][:].rearrange("p j t -> p (j t)"),
+            )
+            nc.sync.dma_start(out_words[:, halves[h]], out_codes[:, halves[h]])
+        for q in range(QUADS):
+            queue = nc.sync if q % 2 else nc.scalar
+            queue.dma_start(out_2[0, 4 * q : 4 * q + 4, :].bitcast(I32), out_scales[32 * q : 32 * q + 4, :].bitcast(I32))

@@ -158,9 +158,12 @@ def tile_picked_selfthreekindpolar_none_po_kernel(
         z2_codes = sb("z2_codes", [P, S], U32)
         z2_scales = sb("z2_scales", [P, S], U8)
 
+        def scale_a(t):
+            nc.scalar.activation(a_scaled[t][:], a[t][:], ACT.Copy, scale=gb_abs[:, t : t + 1])
+
         def look_n4(t):
             nc.vector.tensor_tensor(a[t][:], tab_win[t][:].indirect(n4_sb[:]), y_win[t][:, 0:S], ALU.add)
-            nc.scalar.activation(a_scaled[t][:], a[t][:], ACT.Copy, scale=gb_abs[:, t : t + 1])
+            scale_a(t)
 
         def look_n5(t):
             nc.vector.tensor_tensor(excess[t][:], y_win[t][:].indirect(n5_sb[:]), a[t][:], ALU.subtract)
@@ -214,9 +217,12 @@ def tile_picked_selfthreekindpolar_none_po_kernel(
         lift0 = sb("lift0", [P, S], F32)
         su0_turned = sb("su0_turned", [P, S], F32)
 
+        tab_n4 = sb("tab_n4", [P, S], F32)
+        nc.vector.tensor_copy(tab_n4[:], tab_win[0][:].indirect(n4_sb[:]))
         y_out(1)
         y_out(2)
-        look_n4(0)
+        nc.vector.tensor_tensor(a[0][:], tab_n4[:], y_win[0][:, 0:S], ALU.add)
+        scale_a(0)
         look_n1(0)
         nc.scalar.activation(st0[:], nst_win[0][:, 0:S], ACT.Copy, scale=-1.0)
         y_out(3)
@@ -261,29 +267,26 @@ def tile_picked_selfthreekindpolar_none_po_kernel(
 
         z_in = [sb(f"z_in{i}", [P, 2, P, PACK], BF16) for i in range(2)]
         z_parts = [z_rows[h][:].rearrange("p t (m u) -> p u m t", u=PACK) for h in range(2)]
-        places = [slice(0, P // 2), slice(P // 2, P)]
-
-        def deal_by_scalar(h, i):
+        for i in range(2):
             nc.scalar.copy(
-                z_in[i][:, :, places[h], :].rearrange("p u m t -> p m t u"),
-                z_parts[h][:, 2 * i : 2 * i + 2].rearrange("p u m t -> p m t u"),
+                z_in[i][:, :, 0 : P // 2, :].rearrange("p u m t -> p m t u"),
+                z_parts[0][:, 2 * i : 2 * i + 2].rearrange("p u m t -> p m t u"),
             )
-
-        deal_by_scalar(0, 0)
-        deal_by_scalar(0, 1)
         for t in tiles:
             look_n3(t, 1)
-        for u in range(2):
-            nc.vector.tensor_copy(z_in[0][:, u, places[1], :], z_parts[1][:, u])
-        deal_by_scalar(1, 1)
 
         z_codes = [sb(f"z_codes{u}", [P, P], U32) for u in tiles]
         z_scales = [sb(f"z_scales{u}", [P, P], U8) for u in tiles]
         s_win = [sb(f"s_win{t}", [P, S], F32) for t in tiles]
-        for u in tiles:
-            nc.vector.quantize_mx(
-                out=z_codes[u][:].bitcast(FP8X4), scales=z_scales[u][:], in_=z_in[u // 2][:, u % 2].rearrange("p m t -> p (m t)")
-            )
+        for i in range(2):
+            for u in range(2):
+                nc.vector.tensor_copy(z_in[i][:, u, P // 2 :, :], z_parts[1][:, 2 * i + u])
+            for u in range(2):
+                nc.vector.quantize_mx(
+                    out=z_codes[2 * i + u][:].bitcast(FP8X4),
+                    scales=z_scales[2 * i + u][:],
+                    in_=z_in[i][:, u].rearrange("p m t -> p (m t)"),
+                )
         s_first = [bank(number, f"s_first{h}") for h, number in enumerate((6, 0))]
         for h in range(2):
             product(s_first[h][:, 0:HALF], z_codes[0][:], z_scales[0][:], z2_codes[:, halves[h]], z2_scales[:, halves[h]])

from contextlib import ExitStack

import concourse.mybir as mybir
from concourse.masks import make_identity

K, T, S, H, W = 512, 2048, 512, 512, 256
P = 128
PACK = 4
HALF = S // 2
LIST_ROWS = 16
QUADS = 4
X_EARLY = 512
VECTOR_COLUMNS = 320
FLOPS = 2 * K * H * S + 2 * H * S * S

F32 = mybir.dt.float32
BF16 = mybir.dt.bfloat16
I32 = mybir.dt.int32
U32 = mybir.dt.uint32
U16 = mybir.dt.uint16
U8 = mybir.dt.uint8
FP8X4 = mybir.dt.float8_e4m3fn_x4
ALU = mybir.AluOpType
ACT = mybir.ActivationFunctionType


def tile_picked_selfthreekindpolar_none_po_kernel(
    tc, x_words, x_scales, w1_words, w1_scales, tab, ga, gb, offs, n1, n2, n3, n4, n5, n6, n7, out_0, out_1, out_2
):
    nc = tc.nc
    tiles = range(PACK)
    last = PACK - 1
    halves = [slice(0, HALF), slice(HALF, S)]
    list_halves = [slice(0, HALF // LIST_ROWS), slice(HALF // LIST_ROWS, S // LIST_ROWS)]
    blocks = [slice(b * P, (b + 1) * P) for b in tiles]

    with ExitStack() as ctx:
        keep = ctx.enter_context(tc.tile_pool(name="keep", bufs=1))
        psum = ctx.enter_context(tc.psum_pool(name="psum", bufs=1))

        def sb(name, shape, dtype, reuse=None):
            return keep.tile(shape, dtype, name=name, tag=reuse or name, align_bytes=64)

        def bank(number, name):
            return psum.tile([P, S], F32, name=name, tag=f"bank{number}")

        def product(out, stationary, stationary_scales, moving, moving_scales):
            nc.tensor.matmul_mx(
                out=out,
                lhsT=stationary.bitcast(FP8X4),
                lhsT_scale=stationary_scales,
                rhs=moving.bitcast(FP8X4),
                rhs_scale=moving_scales,
                start=True,
                stop=True,
            )

        def add_turned(out, first, second):
            nc.tensor.matmul(out, first, ident[:], start=True, stop=False, is_transpose=True)
            nc.tensor.matmul(out, second, ident[:], start=False, stop=True, is_transpose=True)

        offs_sb, n1_sb, n2_sb, n3_sb, n4_sb, n5_sb, n6_sb, n7_sb = [
            sb(name, list(src.shape), U16)
            for name, src in (
                ("offs_sb", offs), ("n1_sb", n1), ("n2_sb", n2), ("n3_sb", n3),
                ("n4_sb", n4), ("n5_sb", n5), ("n6_sb", n6), ("n7_sb", n7),
            )
        ]
        xw = sb("xw", [P, T], I32)
        xs = sb("xs", [P, T], U8)
        ww = sb("ww", [P, H], I32)
        ws = sb("ws", [P, H], U8)
        ga_sb = sb("ga_sb", [P, PACK], F32)
        gb_sb = sb("gb_sb", [P, PACK], F32)
        y_win = [sb(f"y_win{t}", [P, 2 * S], F32) for t in tiles]
        tab_win = [sb(f"tab_win{t}", [P, 2 * S], F32) for t in tiles]
        nst_win = [sb(f"nst_win{t}", [P, 2 * S], F32) for t in tiles]
        y_copy = [nst_win[t][:, S:] for t in tiles]
        x_rows = x_words[0].rearrange("p n r -> p (n r)").bitcast(I32)
        tab_rows = tab.rearrange("(p t) j -> t p j", t=PACK)

        nc.gpsimd.memset(xs[:].bitcast(I32), 0)
        nc.vector.memset(ws[:].bitcast(I32), 0)
        nc.sync.dma_start(offs_sb[:], offs)
        nc.sync.dma_start(ww[:], w1_words[0].rearrange("p n r -> p (n r)").bitcast(I32))
        nc.sync.dma_start(xw[:, 0:X_EARLY], x_rows[:, 0:X_EARLY])
        for q in range(QUADS):
            nc.sync.dma_start(xs[32 * q : 32 * q + 4, :].bitcast(I32), x_scales[0, 4 * q : 4 * q + 4, :].bitcast(I32))
        nc.sync.dma_start(xw[:, X_EARLY:], x_rows[:, X_EARLY:])
        for q in range(QUADS):
            nc.sync.dma_start(ws[32 * q : 32 * q + 4, :].bitcast(I32), w1_scales[0, 4 * q : 4 * q + 4, :].bitcast(I32))
        nc.sync.dma_start(tab_win[0][:, 0:S], tab_rows[0])
        nc.sync.dma_start(n4_sb[:], n4)
        nc.sync.dma_start(n1_sb[:], n1)
        nc.sync.dma_start(n5_sb[:], n5)
        nc.sync.dma_start(tab_win[1][:, 0:S], tab_rows[1])
        nc.sync.dma_start(n2_sb[:], n2)
        for t in range(2, PACK):
            nc.sync.dma_start(tab_win[t][:, 0:S], tab_rows[t])
        nc.sync.dma_start(n3_sb[:], n3)
        nc.sync.dma_start(n6_sb[:], n6)
        nc.sync.dma_start(n7_sb[:], n7)
        nc.gpsimd.dma_start(gb_sb[:], gb.rearrange("(p t) o -> p (t o)", t=PACK))
        nc.gpsimd.dma_start(ga_sb[:], ga.rearrange("(p t) o -> p (t o)", t=PACK))
        nc.vector.memset(y_win[0][:, S:], 0.0)
        nc.scalar.copy(tab_win[0][:, S:], y_win[0][:, S:])
        for t in range(1, PACK):
            nc.scalar.copy(y_win[t][:, S:], y_win[0][:, S:])
            nc.scalar.copy(tab_win[t][:, S:], y_win[0][:, S:])

        ident = sb("ident", [P, P], F32)
        gb_step, gb_sign, gb_abs, ga_signed, ga_half, ga_neg, ga_neg_half = [
            sb(name, [P, PACK], F32)
            for name in ("gb_step", "gb_sign", "gb_abs", "ga_signed", "ga_half", "ga_neg", "ga_neg_half")
        ]
        make_identity(nc, ident[:])
        nc.gpsimd.tensor_scalar(gb_step[:], gb_sb[:], 0.0, 2.0, ALU.is_ge, ALU.mult)
        nc.gpsimd.tensor_scalar(gb_sign[:], gb_step[:], 1.0, -1.0, ALU.mult, ALU.add)
        nc.gpsimd.tensor_tensor(gb_abs[:], gb_sb[:], gb_sign[:], ALU.mult)
        nc.gpsimd.tensor_tensor(ga_signed[:], ga_sb[:], gb_sign[:], ALU.mult)
        nc.gpsimd.tensor_scalar(ga_half[:], ga_signed[:], 0.5, 0.0, ALU.mult, ALU.add)
        nc.gpsimd.tensor_scalar(ga_neg[:], ga_signed[:], -1.0, 0.0, ALU.mult, ALU.add)
        nc.gpsimd.tensor_scalar(ga_neg_half[:], ga_signed[:], -0.5, 0.0, ALU.mult, ALU.add)

        picked = sb("picked", [P, S], U32)
        picked_scales = sb("picked_scales", [P, S], U8)
        w_dealt = sb("w_dealt", [P, PACK, P], I32)
        ws_first = sb("ws_first", [P, P], U8)
        ws_rest = sb("ws_rest", [P, last, P], U8)
        ws_by_tile = ws[:].rearrange("p (m t) -> p t m", t=PACK)
        nc.vector.tensor_copy(picked_scales[:], xs[:].indirect(offs_sb[:]))
        nc.vector.tensor_copy(w_dealt[:], ww[:].rearrange("p (m t) -> p t m", t=PACK))
        y_first = [bank(h, f"y_first{h}") for h in range(2)]
        nc.vector.tensor_copy(picked[:, halves[0]], xw[:].bitcast(U32).indirect(offs_sb[:, list_halves[0]]))
        nc.vector.tensor_copy(ws_first[:], ws_by_tile[:, 0])
        product(y_first[0][:, 0:HALF], w_dealt[:, 0], ws_first[:], picked[:, halves[0]], picked_scales[:, halves[0]])
        nc.scalar.copy(y_win[0][:, halves[0]], y_first[0][:, 0:HALF])
        nc.vector.tensor_copy(picked[:, halves[1]], xw[:].bitcast(U32).indirect(offs_sb[:, list_halves[1]]))
        product(y_first[1][:, 0:HALF], w_dealt[:, 0], ws_first[:], picked[:, halves[1]], picked_scales[:, halves[1]])
        nc.scalar.copy(y_win[0][:, halves[1]], y_first[1][:, 0:HALF])
        for h in range(2):
            nc.scalar.copy(y_copy[0][:, halves[h]], y_first[h][:, 0:HALF])
        nc.vector.tensor_copy(ws_rest[:], ws_by_tile[:, 1:])
        y_ps = {t: bank(t + 1, f"y_ps{t}") for t in range(1, PACK)}
        for t in range(1, PACK):
            product(y_ps[t][:], w_dealt[:, t], ws_rest[:, t - 1], picked[:], picked_scales[:])

        def y_out(t):
            nc.scalar.copy(y_win[t][:, 0:S], y_ps[t][:])
            nc.sync.dma_start(y_copy[t], y_win[t][:, 0:S])

        a = [sb(f"a{t}", [P, S], F32) for t in tiles]
        a_scaled = [sb(f"a_scaled{t}", [P, S], F32) for t in tiles]
        excess = [sb(f"excess{t}", [P, S], F32) for t in tiles]
        excess_scaled = [sb(f"excess_scaled{t}", [P, S], F32) for t in tiles]
        z2_sum = [bank((5 + b) % 8, f"z2_sum{b}") for b in tiles]
        z2_in = sb("z2_in", [P, S, PACK], BF16)
        z2_codes = sb("z2_codes", [P, S], U32)
        z2_scales = sb("z2_scales", [P, S], U8)

        def scale_a(t):
            nc.scalar.activation(a_scaled[t][:], a[t][:], ACT.Copy, scale=gb_abs[:, t : t + 1])

        def look_n4(t):
            nc.vector.tensor_tensor(a[t][:], tab_win[t][:].indirect(n4_sb[:]), y_win[t][:, 0:S], ALU.add)
            scale_a(t)

        def look_n5(t):
            nc.vector.tensor_tensor(excess[t][:], y_win[t][:].indirect(n5_sb[:]), a[t][:], ALU.subtract)

        def z2_add(t):
            nc.scalar.activation(excess_scaled[t][:], excess[t][:], ACT.Relu, scale=gb_abs[:, t : t + 1])
            for b in tiles:
                add_turned(z2_sum[b][:, blocks[t]], a_scaled[t][:, blocks[b]], excess_scaled[t][:, blocks[b]])

        def z2_turn_back(h):
            turned = sb(f"z2_turned{h}", [P, 2, S], BF16)
            back = bank(5 + 2 * h, f"z2_back{h}")
            for b in range(2):
                nc.scalar.copy(
                    turned[:, b, :].rearrange("j (u p e) -> j u p e", u=2, e=2),
                    z2_sum[2 * h + b][:].rearrange("j (u e p) -> j u p e", u=2, e=2),
                )
                words = turned[:, b, :].bitcast(F32)
                for u in range(2):
                    nc.tensor.transpose(back[:, blocks[2 * b + u]], words[:, blocks[u]], ident[:])
            z2_words = z2_in[:, halves[h], :].rearrange("p j t -> p (j t)").bitcast(F32)
            nc.scalar.copy(
                z2_words.rearrange("p (b j u) -> p b j u", b=2, u=2),
                back[:].rearrange("p (b u j) -> p b j u", b=2, u=2),
            )

        su_half = [sb(f"su_half{t}", [P, S], F32) for t in tiles]
        su_full = [sb(f"su_full{t}", [P, S], F32) for t in tiles]
        z_rows = [sb(f"z_rows{h}", [P, PACK, HALF], F32) for h in range(2)]
        nst_n2 = {}

        def look_n1(t):
            nc.vector.tensor_tensor(nst_win[t][:, 0:S], y_win[t][:].indirect(n1_sb[:]), y_copy[t], ALU.subtract)

        def look_n2(t, reuse=None):
            nst_n2[t] = sb(f"nst_n2_{t}", [P, S], F32, reuse)
            nc.vector.tensor_copy(nst_n2[t][:], nst_win[t][:].indirect(n2_sb[:]))

        def su_by_vector(t, nsu):
            nc.vector.tensor_tensor(nsu, nst_win[t][:, 0:S], nst_n2[t][:], ALU.min)
            nc.scalar.activation(su_half[t][:], nsu, ACT.Copy, scale=ga_neg_half[:, t : t + 1])
            nc.scalar.activation(su_full[t][:], nsu, ACT.Copy, scale=ga_neg[:, t : t + 1])

        def look_n3(t, h):
            nc.vector.tensor_tensor(
                z_rows[h][:, t, :], su_half[t][:].indirect(n3_sb[:, list_halves[h]]), su_full[t][:, halves[h]], ALU.add
            )

        st0 = sb("st0", [P, S], F32)
        deficit0 = sb("deficit0", [P, S], F32)
        lift0 = sb("lift0", [P, S], F32)
        su0_turned = sb("su0_turned", [P, S], F32)

        tab_n4 = sb("tab_n4", [P, S], F32)
        nc.vector.tensor_copy(tab_n4[:], tab_win[0][:].indirect(n4_sb[:]))
        y_out(1)
        y_out(2)
        nc.vector.tensor_tensor(a[0][:], tab_n4[:], y_win[0][:, 0:S], ALU.add)
        scale_a(0)
        look_n1(0)
        nc.scalar.activation(st0[:], nst_win[0][:, 0:S], ACT.Copy, scale=-1.0)
        y_out(3)
        look_n4(1)
        look_n5(0)
        z2_add(0)
        nc.vector.tensor_tensor(deficit0[:], nst_win[0][:].indirect(n2_sb[:]), st0[:], ALU.add)
        nc.scalar.activation(lift0[:], deficit0[:], ACT.Relu, scale=-1.0)
        su0_sum = bank(1, "su0_sum")
        for b in tiles:
            add_turned(su0_sum[:, blocks[b]], st0[:, blocks[b]], lift0[:, blocks[b]])
        look_n5(1)
        z2_add(1)
        look_n4(2)
        su0_back = bank(2, "su0_back")
        nc.scalar.copy(su0_turned[:], su0_sum[:])
        for b in tiles:
            nc.tensor.transpose(su0_back[:, blocks[b]], su0_turned[:, blocks[b]], ident[:])
        look_n1(1)
        look_n5(2)
        nc.scalar.activation(su_half[0][:], su0_back[:], ACT.Copy, scale=ga_half[:, 0:1])
        nc.scalar.activation(su_full[0][:], su0_back[:], ACT.Copy, scale=ga_signed[:, 0:1])
        z2_add(2)
        look_n4(3)
        look_n2(1)
        look_n5(3)
        z2_add(3)
        look_n1(2)
        z2_turn_back(0)
        look_n1(3)
        su_by_vector(1, sb("nsu1", [P, S], F32, f"excess_scaled{last}")[:])
        z2_turn_back(1)
        look_n2(2, f"a_scaled{last}")
        look_n2(3, "z2_turned0")
        su_by_vector(2, sb("nsu2", [P, S], F32)[:])
        look_n3(0, 0)
        su_by_vector(3, z_rows[1][:].rearrange("p t j -> p (t j)")[:, S:])
        look_n3(1, 0)
        look_n3(2, 0)
        nc.vector.quantize_mx(out=z2_codes[:].bitcast(FP8X4), scales=z2_scales[:], in_=z2_in[:].rearrange("p j t -> p (j t)"))
        look_n3(3, 0)

        z_in = [sb(f"z_in{i}", [P, 2, P, PACK], BF16) for i in range(2)]
        z_parts = [z_rows[h][:].rearrange("p t (m u) -> p u m t", u=PACK) for h in range(2)]
        for i in range(2):
            nc.scalar.copy(
                z_in[i][:, :, 0 : P // 2, :].rearrange("p u m t -> p m t u"),
                z_parts[0][:, 2 * i : 2 * i + 2].rearrange("p u m t -> p m t u"),
            )
        for t in tiles:
            look_n3(t, 1)

        z_codes = [sb(f"z_codes{u}", [P, P], U32) for u in tiles]
        z_scales = [sb(f"z_scales{u}", [P, P], U8) for u in tiles]
        s_win = [sb(f"s_win{t}", [P, S], F32) for t in tiles]
        for i in range(2):
            for u in range(2):
                nc.vector.tensor_copy(z_in[i][:, u, P // 2 :, :], z_parts[1][:, 2 * i + u])
            for u in range(2):
                nc.vector.quantize_mx(
                    out=z_codes[2 * i + u][:].bitcast(FP8X4),
                    scales=z_scales[2 * i + u][:],
                    in_=z_in[i][:, u].rearrange("p m t -> p (m t)"),
                )
        s_first = [bank(number, f"s_first{h}") for h, number in enumerate((6, 0))]
        for h in range(2):
            product(s_first[h][:, 0:HALF], z_codes[0][:], z_scales[0][:], z2_codes[:, halves[h]], z2_scales[:, halves[h]])
        nc.scalar.activation(s_win[0][:, halves[0]], s_first[0][:, 0:HALF], ACT.Copy, scale=0.0625)
        nc.vector.tensor_scalar(s_win[0][:, halves[1]], s_first[1][:, 0:HALF], 0.0625, None, ALU.mult)
        for t, number in zip(range(1, PACK), (5, 7, 1)):
            s_ps = bank(number, f"s_ps{t}")
            product(s_ps[:], z_codes[t][:], z_scales[t][:], z2_codes[:], z2_scales[:])
            nc.scalar.activation(s_win[t][:], s_ps[:], ACT.Copy, scale=0.0625)

        pa_neg_half = [sb(f"pa_neg_half{t}", [P, W], F32) for t in tiles]
        pb = [sb(f"pb{t}", [P, W], F32) for t in tiles]
        pa_square = [sb(f"pa_square{t}", [P, W], F32) for t in tiles]
        pb_square = [sb(f"pb_square{t}", [P, W], F32) for t in tiles]
        ra_turned = [sb(f"ra_turned{t}", [P, W], F32) for t in tiles]
        ra = [sb(f"ra{t}", [P, W], F32) for t in tiles]
        out_win = [sb(f"out_win{t}", [P, S], F32) for t in tiles]
        out_rows = out_0.rearrange("(p t) j -> t p j", t=PACK)
        ra_ps = {}

        def look_pairs(t):
            nc.vector.tensor_scalar(pa_neg_half[t][:], s_win[t][:].indirect(n6_sb[:]), -0.5, 0.0, ALU.mult, ALU.add)
            nc.vector.tensor_copy(pb[t][:], s_win[t][:].indirect(n7_sb[:]))
            nc.scalar.activation(pa_square[t][:], pa_neg_half[t][:], ACT.Square, scale=2.0)
            nc.scalar.activation(pb_square[t][:], pb[t][:], ACT.Square)

        def root(t):
            squares = bank((2, 4)[t % 2], f"squares{t}")
            ra_ps[t] = bank((3, 6)[t % 2], f"ra_ps{t}")
            for b in range(W // P):
                add_turned(squares[:, blocks[b]], pa_square[t][:, blocks[b]], pb_square[t][:, blocks[b]])
            nc.scalar.activation(ra_turned[t][:], squares[:, 0:W], ACT.Sqrt, bias=0.25)
            for b in range(W // P):
                nc.tensor.transpose(ra_ps[t][:, blocks[b]], ra_turned[t][:, blocks[b]], ident[:])

        def root_out(t):
            nc.scalar.copy(ra[t][:], ra_ps[t][:, 0:W])

        def put_rb(t):
            nc.vector.tensor_tensor(out_win[t][:].indirect(n7_sb[:]), pb[t][:], pa_neg_half[t][:], ALU.add)

        look_pairs(0)
        for t in range(last):
            look_pairs(t + 1)
            root(t)
            put_rb(t)
            root_out(t)
        root(last)
        root_out(last)
        put_rb(last)

        out_bf16 = sb("out_bf16", [P, PACK, S], BF16, f"ra_turned{last}")
        for t in tiles:
            nc.vector.tensor_copy(out_win[t][:].indirect(n6_sb[:]), ra[t][:])
            nc.sync.dma_start(out_rows[t], out_win[t][:])
            if t < last:
                nc.scalar.copy(out_bf16[:, t, :], out_win[t][:])

        out_in = [sb(f"out_in{h}", [P, HALF, PACK], BF16) for h in range(2)]
        out_codes = sb("out_codes", [P, S], I32)
        out_scales = sb("out_scales", [P, S], U8)
        out_words = out_1[0].rearrange("p n r -> p (n r)").bitcast(I32)

        def interleave(copy, h, start, stop):
            copy(
                out_in[h][:, start - h * HALF : stop - h * HALF, :].rearrange("p (c i) t -> p c t i", i=4),
                out_bf16[:, :, start:stop].rearrange("p t (c i) -> p c t i", i=4),
            )

        nc.vector.tensor_copy(out_bf16[:, last, 0:VECTOR_COLUMNS], out_win[last][:, 0:VECTOR_COLUMNS])
        nc.scalar.copy(out_bf16[:, last, VECTOR_COLUMNS:], out_win[last][:, VECTOR_COLUMNS:])
        interleave(nc.vector.tensor_copy, 0, 0, HALF)
        interleave(nc.vector.tensor_copy, 1, HALF, VECTOR_COLUMNS)
        interleave(nc.scalar.copy, 1, VECTOR_COLUMNS, S)
        for h in range(2):
            nc.vector.quantize_mx(
                out=out_codes[:, halves[h]].bitcast(FP8X4),
                scales=out_scales[:, halves[h]],
                in_=out_in[h][:].rearrange("p j t -> p (j t)"),
            )
            nc.sync.dma_start(out_words[:, halves[h]], out_codes[:, halves[h]])
        for q in range(QUADS):
            queue = nc.sync if q % 2 else nc.scalar
            queue.dma_start(out_2[0, 4 * q : 4 * q + 4, :].bitcast(I32), out_scales[32 * q : 32 * q + 4, :].bitcast(I32))
